import numpy as np
import ml_dtypes


def mxq(x, axis, fmt="e4m3"):
    dtype, down = {"e4m3": (ml_dtypes.float8_e4m3fn, 7), "e5m2": (ml_dtypes.float8_e5m2, 14)}[fmt]
    v = np.moveaxis(np.asarray(x, np.float32).astype(ml_dtypes.bfloat16).astype(np.float64), axis, -1)
    blocks = v.reshape(v.shape[:-1] + (-1, 32))
    amax = np.abs(blocks).max(-1, keepdims=True)
    byte = np.maximum(np.where(amax > 0, np.frexp(amax)[1] - 1 + 127, 0) - down, 1)
    scale = np.exp2(byte - 127.0)
    codes = (blocks / scale).astype(np.float32).astype(dtype).astype(np.float64)
    return np.moveaxis((codes * scale).reshape(v.shape), -1, axis)


WIDE = False


def mx_kscale(k):
    if not WIDE:
        return np.ones(k)
    levels = np.array([10, -10, 5, -5, 0])
    if k % 512:
        return np.exp2(np.random.permutation(np.resize(levels, k // 32))).repeat(32)
    a = np.empty((k // 512, 16))
    for p in range(k // 512):
        a[p, :8] = np.random.permutation(np.resize(levels, 8))
        for g in range(8):
            far = levels[np.abs(levels - a[p, g]) >= 10]
            a[p, g + 8] = far[np.random.randint(len(far))]
    return np.exp2(a.ravel()).repeat(32)


def f64(x):
    return np.asarray(x).astype(np.float64)


def striped(idx):
    return np.tile(idx.reshape(-1, 16).T, (8, 1)).astype(np.uint16)


def unstriped(offs):
    return offs[:16].T.reshape(-1).astype(np.int64)


E2M1 = np.array([0.0, 0.5, 1.0, 1.5, 2.0, 3.0, 4.0, 6.0, -0.0, -0.5, -1.0, -1.5, -2.0, -3.0, -4.0, -6.0])


def pack_weight(w, fmt):
    k, n = w.shape
    w = f64(np.asarray(w, np.float32).astype(ml_dtypes.bfloat16)).reshape(k // 32, 32, n)
    amax = np.abs(w).max(1)
    if fmt == "e4m3":
        byte = np.frexp(amax)[1] - 1 + 127 - 7
    else:
        mant, ex = np.frexp(amax / 6.0)
        byte = np.where(mant > 0.5, ex, ex - 1) + 127
    byte = np.clip(np.where(amax > 0, byte, 1), 1, 254)
    scaled = (w * np.exp2(127.0 - byte)[:, None, :]).reshape(k, n).astype(np.float32)
    by_word = np.ascontiguousarray(scaled.reshape(k // 512, 128, 4, n).transpose(0, 1, 3, 2))
    if fmt == "e4m3":
        words = by_word.astype(ml_dtypes.float8_e4m3fn).view(np.uint8)
    else:
        c = by_word.astype(ml_dtypes.float4_e2m1fn).view(np.uint8) & 0xF
        words = (c[..., 0::2] | (c[..., 1::2] << 4)).reshape(k // 512, 128, 2 * n)
    return np.ascontiguousarray(words), np.ascontiguousarray(byte.astype(np.uint8).reshape(k // 512, 16, n))


def unpack_weight(words, scales, fmt):
    g, _, n = scales.shape
    words = np.ascontiguousarray(words).reshape(g, 128, n, -1)
    if fmt == "e4m3":
        vals = words.view(ml_dtypes.float8_e4m3fn).astype(np.float64)
    else:
        nib = np.empty((g, 128, n, 4), np.uint8)
        nib[..., 0::2] = words & 0xF
        nib[..., 1::2] = words >> 4
        vals = E2M1[nib]
    vals = vals * np.repeat(np.exp2(scales.astype(np.float64) - 127.0), 8, axis=1)[..., None]
    return vals.transpose(0, 1, 3, 2).reshape(g * 512, n)


def gelu(v):
    return 0.5 * v * (1.0 + np.tanh(np.sqrt(2.0 / np.pi) * (v + 0.044715 * v**3)))


def striped8(idx):
    return np.concatenate([v.reshape(-1, 16).T for v in idx]).astype(np.uint16)


def unstriped8(offs):
    return np.stack([offs[16 * g:16 * g + 16].T.reshape(-1) for g in range(8)]).astype(np.int64)


def heads(xT, wgt, idx8):
    k = np.arange(xT.shape[0])
    return wgt[k // 4 % 128] * xT[k[:, None], idx8[k % 512 // 64]]


K, M, H, N, T, P, S = 1024, 512, 1024, 256, 2048, 2048, 1024

def setup_inputs():
    n = np.random.standard_normal
    s = mx_kscale(K)[:, None]
    s2 = mx_kscale(M)[:, None]
    u = mx_kscale(H)[:, None]
    tab_words, tab_scales = pack_weight(n((M, T)) * s2, "e4m3")
    wr_words, wr_scales = pack_weight(n((M, H)) / np.sqrt(M) / s2, "e2m1")
    return {
        "xT": (n((K, P)) * s).astype(np.float32),
        "wgt": np.repeat(np.random.uniform(0.5, 2.0, (8, S)), 16, axis=0).astype(np.float32),
        "offs2": striped8(np.stack([np.random.permutation(P)[:S] for _ in range(8)])),
        "tab_words": tab_words, "tab_scales": tab_scales,
        "offs": striped(np.random.permutation(T)[:S]),
        "wk": (0.8 * n((K, H)) / np.sqrt(K) / s).astype(np.float32),
        "wr_words": wr_words, "wr_scales": wr_scales,
        "gain": (np.exp(0.3 * n(H)) * u[:, 0]).astype(np.float32),
        "wo": (n((H, N)) / np.sqrt(H) / u).astype(np.float32),
    }

def reference(xT, wgt, offs2, tab_words, tab_scales, offs, wk, wr_words, wr_scales, gain, wo):
    xg = mxq(heads(f64(xT), f64(wgt), unstriped8(offs2)), 0, "e4m3")
    v = unpack_weight(tab_words, tab_scales, "e4m3")[:, unstriped(offs)]
    wkq = mxq(f64(wk), 0, "e4m3")
    wr = unpack_weight(wr_words, wr_scales, "e2m1")
    a = wkq.T @ xg
    b = wr.T @ v
    d = np.abs(a - b)
    h = f64(gain)[:, None] * np.log(1.0 + d)
    hq = mxq(h, 0, "e4m3")
    woq = mxq(f64(wo), 0, "e4m3")
    return woq.T @ hq

@@ -1,0 +1,318 @@
+from contextlib import ExitStack
+
+import concourse.mybir as mybir
+
+K, M, H, N, T, S = 1024, 512, 1024, 256, 2048, 1024
+FLOPS = 2 * S * (K * H + M * H + H * N)
+
+F32 = mybir.dt.float32
+BF16 = mybir.dt.bfloat16
+I32 = mybir.dt.int32
+U32 = mybir.dt.uint32
+U16 = mybir.dt.uint16
+U8 = mybir.dt.uint8
+FP8X4 = mybir.dt.float8_e4m3fn_x4
+FP4X4 = mybir.dt.float4_e2m1fn_x4
+ACT = mybir.ActivationFunctionType
+MULT = mybir.AluOpType.mult
+
+P = 128
+PACK = 4
+PASS = P * PACK
+HALF = 512
+LIST_COLS = HALF // 16
+
+
+def tile_list_motif_variant_evidence_kernel(
+    tc, xT, wgt, offs2, tab_words, tab_scales, offs, wk, wr_words, wr_scales, gain, wo, out
+):
+    nc = tc.nc
+    with ExitStack() as ctx:
+        keep = ctx.enter_context(tc.tile_pool(name="keep", bufs=1))
+        ring = ctx.enter_context(tc.tile_pool(name="ring", bufs=4))
+        diff_banks = ctx.enter_context(tc.psum_pool(name="diff_banks", bufs=6))
+        out_banks = ctx.enter_context(tc.psum_pool(name="out_banks", bufs=2))
+
+        def held(shape, dtype, name):
+            return keep.tile(shape, dtype, name=name, align_bytes=64)
+
+        x_list = keep.tile([P, S // 16], U16, name="x_list")
+        tab_list = keep.tile([P, S // 16], U16, name="tab_list")
+        wgt_sb = held([P, S], F32, "wgt_sb")
+        planes = [[held([P, T], F32, f"plane{a}{i}") for i in range(PACK)] for a in range(2)]
+        tab_w = held([P, T], I32, "tab_w")
+        tab_s = held([P, T // 4], I32, "tab_s")
+        wr_w_raw = held([P, H // 2], I32, "wr_w_raw")
+        wr_s_raw = held([P, H // 4], I32, "wr_s_raw")
+        wr_w = held([P, 2 * H], U8, "wr_w")
+        wr_s = held([P, H], U8, "wr_s")
+        v_w = held([P, S], U32, "v_w")
+        v_s = held([P, S], U8, "v_s")
+        gain_sb = held([P, 2, PACK], F32, "gain_sb")
+        ones = held([P, 1], F32, "ones")
+        warm = held([P, 1], F32, "warm")
+        wo_raw = held([P, 2, PACK, N], F32, "wo_raw")
+        wo_w = held([P, 2, N], U32, "wo_w")
+        wo_s = held([P, 2, N], U8, "wo_s")
+        xg_w = [[held([P, HALF], U32, f"xg_w{a}{j}") for j in range(2)] for a in range(2)]
+        xg_s = [[held([P, HALF], U8, f"xg_s{a}{j}") for j in range(2)] for a in range(2)]
+        wk_w = [[held([P, HALF], U32, f"wk_w{a}{r}") for r in range(2)] for a in range(2)]
+        wk_s = [[held([P, HALF], U8, f"wk_s{a}{r}") for r in range(2)] for a in range(2)]
+        h_w = [[held([P, HALF], U32, f"h_w{r}{j}") for j in range(2)] for r in range(2)]
+        h_s = [[held([P, HALF], U8, f"h_s{r}{j}") for j in range(2)] for r in range(2)]
+        wk_raw = {}
+        picked = {}
+        grouped = {}
+        mags = {}
+        damped = {}
+
+        def load_plane(a, i):
+            rows = xT[a * PASS : (a + 1) * PASS, :].rearrange("(p i) t -> i p t", i=PACK)
+            nc.sync.dma_start(out=planes[a][i][:], in_=rows[i])
+
+        def load_wk(a, r):
+            wk_raw[a, r] = ring.tile([P, PACK, HALF], F32, name=f"wk_raw{a}{r}", tag="wide_b", align_bytes=64)
+            rows = wk[a * PASS : (a + 1) * PASS, r * HALF : (r + 1) * HALF]
+            nc.sync.dma_start(out=wk_raw[a, r][:], in_=rows.rearrange("(p i) c -> p i c", i=PACK))
+
+        def load_scale_rows(tile, rows):
+            for q in range(4):
+                nc.scalar.dma_start(out=tile[32 * q : 32 * q + 4, :], in_=rows[0, 4 * q : 4 * q + 4, :].bitcast(I32))
+
+        def cast(engine, out_ap, in_ap, factor):
+            if engine == "scalar":
+                nc.scalar.activation(out_ap, in_ap, ACT.Copy, scale=factor)
+            elif factor == 1.0:
+                nc.vector.tensor_copy(out_ap, in_ap)
+            else:
+                nc.vector.tensor_scalar(out_ap, in_ap, factor, None, MULT)
+
+        def quantize(words, scales, grouped):
+            nc.vector.quantize_mx(out=words.bitcast(FP8X4), scales=scales, in_=grouped)
+
+        def gather_plane(a, i, j):
+            if (a, j) not in picked:
+                picked[a, j] = ring.tile([P, PACK, HALF], F32, name=f"picked{a}{j}", tag="wide_a", align_bytes=64)
+            window = planes[a][i][:].indirect(x_list[:, j * LIST_COLS : (j + 1) * LIST_COLS])
+            nc.vector.tensor_tensor(picked[a, j][:, i, :], window, wgt_sb[:, j * HALF : (j + 1) * HALF], MULT)
+
+        def group_xg(a, j, engine):
+            grouped["xg", a, j] = ring.tile([P, HALF * PACK], BF16, name=f"xg_bf{a}{j}", tag="grouped", align_bytes=64)
+            cast(
+                engine,
+                grouped["xg", a, j][:].rearrange("p (c u i) -> p c i u", u=4, i=PACK),
+                picked[a, j][:].rearrange("p i (c u) -> p c i u", u=4),
+                -1.0,
+            )
+
+        def quantize_xg(a, j):
+            quantize(xg_w[a][j][:], xg_s[a][j][:], grouped["xg", a, j][:])
+
+        def group_wk(a, r, engine):
+            grouped["wk", a, r] = ring.tile([P, HALF * PACK], BF16, name=f"wk_bf{a}{r}", tag="grouped", align_bytes=64)
+            cast(
+                engine,
+                grouped["wk", a, r][:].rearrange("p (t m i) -> p m i t", t=PACK, i=PACK),
+                wk_raw[a, r][:].rearrange("p i (m t) -> p m i t", t=PACK),
+                1.0,
+            )
+
+        def quantize_wk(a, r):
+            quantize(wk_w[a][r][:], wk_s[a][r][:], grouped["wk", a, r][:])
+
+        def group_wo(engine):
+            grouped["wo"] = ring.tile([P, 2, N * PACK], BF16, name="wo_bf", tag="grouped", align_bytes=64)
+            for r in range(2):
+                cast(
+                    engine,
+                    grouped["wo"][:, r, :].rearrange("p (c u i) -> p c i u", u=4, i=PACK),
+                    wo_raw[:, r, :, :].rearrange("p i (c u) -> p c i u", u=4),
+                    1.0,
+                )
+
+        def quantize_wo():
+            quantize(
+                wo_w[:].rearrange("p r n -> p (r n)"),
+                wo_s[:].rearrange("p r n -> p (r n)"),
+                grouped["wo"][:].rearrange("p r c -> p (r c)"),
+            )
+
+        def gather_table_words(j):
+            cols = slice(j * HALF, (j + 1) * HALF)
+            window = tab_w[:].bitcast(U32).indirect(tab_list[:, j * LIST_COLS : (j + 1) * LIST_COLS])
+            nc.vector.tensor_copy(v_w[:, cols], window)
+
+        def difference(r, j, by_pass):
+            sites = slice(j * HALF, (j + 1) * HALF)
+            mags[r, j] = ring.tile([P, PACK, HALF], F32, name=f"mag{r}{j}", tag="wide_a", align_bytes=64)
+            banks = [diff_banks.tile([P, HALF], F32, name=f"diff{r}{j}{t}", tag="diff") for t in range(PACK)]
+
+            def sample_pass(t, a):
+                cols = slice(t * P, (t + 1) * P)
+                nc.tensor.matmul_mx(
+                    out=banks[t][:],
+                    lhsT=wk_w[a][r][:, cols].bitcast(FP8X4),
+                    lhsT_scale=wk_s[a][r][:, cols],
+                    rhs=xg_w[a][j][:].bitcast(FP8X4),
+                    rhs_scale=xg_s[a][j][:],
+                    start=(a == 0),
+                    stop=(a == 1),
+                )
+
+            def motif_pass(t):
+                c0 = r * HALF + t * P
+                nc.tensor.matmul_mx(
+                    out=banks[t][:],
+                    lhsT=wr_w[:, 2 * c0 : 2 * (c0 + P)].bitcast(FP4X4),
+                    lhsT_scale=wr_s[:, c0 : c0 + P],
+                    rhs=v_w[:, sites].bitcast(FP8X4),
+                    rhs_scale=v_s[:, sites],
+                    start=False,
+                    stop=False,
+                )
+
+            steps = [(t, step) for t in range(PACK) for step in range(3)]
+            if by_pass:
+                steps = [(t, step) for step in range(3) for t in range(PACK)]
+            for t, step in steps:
+                if step == 1:
+                    motif_pass(t)
+                else:
+                    sample_pass(t, step // 2)
+                if step == 2:
+                    nc.scalar.activation(mags[r, j][:, t, :], banks[t][:], ACT.Abs)
+
+        def damp(r, j, c0, width):
+            if (r, j) not in damped:
+                damped[r, j] = ring.tile([P, PACK, HALF], F32, name=f"damped{r}{j}", tag="wide_b", align_bytes=64)
+            cols = slice(c0, c0 + width)
+            nc.scalar.activation(damped[r, j][:, :, cols], mags[r, j][:, :, cols], ACT.Ln, bias=ones[:])
+
+        def weigh(r, j, c0, width):
+            if ("h", r, j) not in grouped:
+                grouped["h", r, j] = ring.tile([P, HALF * PACK], BF16, name=f"h_bf{r}{j}", tag="grouped", align_bytes=64)
+            nc.vector.tensor_tensor(
+                grouped["h", r, j][:, PACK * c0 : PACK * (c0 + width)].rearrange("p (c u t) -> p c t u", u=4, t=PACK),
+                damped[r, j][:, :, c0 : c0 + width].rearrange("p t (c u) -> p c t u", u=4),
+                gain_sb[:, r, :].unsqueeze(1).unsqueeze(3).to_broadcast([P, width // 4, PACK, 4]),
+                MULT,
+            )
+
+        def quantize_h(r, j, c0, width):
+            cols = slice(c0, c0 + width)
+            quantize(h_w[r][j][:, cols], h_s[r][j][:, cols], grouped["h", r, j][:, PACK * c0 : PACK * (c0 + width)])
+
+        def evidence(j, c0, width):
+            cols = slice(c0, c0 + width)
+            bank = out_banks.tile([P, 2, 256], F32, name=f"ev{j}_{c0}", tag="ev")
+            for n in range(2):
+                for r in range(2):
+                    nc.tensor.matmul_mx(
+                        out=bank[:, n, :width],
+                        lhsT=wo_w[:, r, n * P : (n + 1) * P].bitcast(FP8X4),
+                        lhsT_scale=wo_s[:, r, n * P : (n + 1) * P],
+                        rhs=h_w[r][j][:, cols].bitcast(FP8X4),
+                        rhs_scale=h_s[r][j][:, cols],
+                        start=(r == 0),
+                        stop=(r == 1),
+                    )
+            staged = ring.tile([P, 2, 256], F32, name=f"staged{j}_{c0}", tag="staged")
+            nc.scalar.copy(staged[:, :, :width], bank[:, :, :width])
+            sites = slice(j * HALF + c0, j * HALF + c0 + width)
+            nc.sync.dma_start(out=out[:, sites].rearrange("(n p) s -> p n s", p=P), in_=staged[:, :, :width])
+
+        nc.vector.memset(tab_s[:], 0)
+        nc.vector.memset(wr_s_raw[:], 0)
+        nc.vector.memset(ones[:], 1.0)
+        load_scale_rows(tab_s, tab_scales)
+        nc.scalar.activation(warm[:], ones[:], ACT.Ln)
+        load_scale_rows(wr_s_raw, wr_scales)
+
+        nc.sync.dma_start(x_list[:], offs2)
+        nc.sync.dma_start(tab_list[:], offs)
+        nc.sync.dma_start(out=wgt_sb[:], in_=wgt)
+        load_plane(0, 0)
+        load_plane(0, 1)
+        nc.sync.dma_start(out=wr_w_raw[:], in_=wr_words[0].bitcast(I32))
+        load_plane(0, 2)
+        load_plane(0, 3)
+        load_wk(0, 0)
+        load_plane(1, 0)
+        load_plane(1, 1)
+        load_wk(1, 0)
+        load_plane(1, 2)
+        load_plane(1, 3)
+        nc.sync.dma_start(out=tab_w[:], in_=tab_words[0].rearrange("p t i -> p (t i)").bitcast(I32))
+        nc.sync.dma_start(out=gain_sb[:], in_=gain.rearrange("(r p t) -> p r t", p=P, t=PACK))
+        load_wk(0, 1)
+        load_wk(1, 1)
+        nc.sync.dma_start(out=wo_raw[:], in_=wo.rearrange("(r p i) n -> p r i n", p=P, i=PACK))
+
+        def both_halves(a, i):
+            gather_plane(a, i, 0)
+            gather_plane(a, i, 1)
+
+        nc.vector.tensor_copy(v_s[:], tab_s[:].bitcast(U8).indirect(tab_list[:]))
+        both_halves(0, 0)
+        both_halves(0, 1)
+        nc.vector.tensor_copy(
+            wr_w[:].bitcast(U16).rearrange("p (r t m) -> p r m t", r=2, t=PACK),
+            wr_w_raw[:].bitcast(U16).rearrange("p (r m t) -> p r m t", r=2, t=PACK),
+        )
+        nc.vector.tensor_copy(
+            wr_s[:].rearrange("p (r t m) -> p r m t", r=2, t=PACK),
+            wr_s_raw[:].bitcast(U8).rearrange("p (r m t) -> p r m t", r=2, t=PACK),
+        )
+        both_halves(0, 2)
+        both_halves(0, 3)
+        group_xg(0, 0, "scalar")
+        group_xg(0, 1, "scalar")
+        group_wk(0, 0, "scalar")
+        group_wk(1, 0, "scalar")
+        both_halves(1, 0)
+        quantize_xg(0, 0)
+        both_halves(1, 1)
+        quantize_xg(0, 1)
+        quantize_wk(0, 0)
+        both_halves(1, 2)
+        quantize_wk(1, 0)
+        both_halves(1, 3)
+        group_xg(1, 0, "scalar")
+        gather_table_words(0)
+        quantize_xg(1, 0)
+        difference(0, 0, True)
+        damp(0, 0, 0, 512)
+        group_xg(1, 1, "vector")
+        gather_table_words(1)
+        quantize_xg(1, 1)
+        difference(0, 1, False)
+        damp(0, 1, 0, 512)
+        group_wk(0, 1, "vector")
+        group_wk(1, 1, "vector")
+        quantize_wk(0, 1)
+        quantize_wk(1, 1)
+        difference(1, 0, False)
+        damp(1, 0, 0, 512)
+        weigh(0, 0, 0, 512)
+        group_wo("vector")
+        quantize_h(0, 0, 0, 512)
+        quantize_wo()
+        weigh(0, 1, 0, 512)
+        difference(1, 1, False)
+        weigh(1, 0, 0, 512)
+        quantize_h(0, 1, 0, 512)
+        quantize_h(1, 0, 0, 512)
+        damp(1, 1, 0, 256)
+        damp(1, 1, 256, 128)
+        damp(1, 1, 384, 128)
+        evidence(0, 0, 256)
+        evidence(0, 256, 256)
+        weigh(1, 1, 0, 256)
+        weigh(1, 1, 256, 128)
+        quantize_h(1, 1, 0, 256)
+        weigh(1, 1, 384, 128)
+        quantize_h(1, 1, 256, 128)
+        quantize_h(1, 1, 384, 128)
+        evidence(1, 0, 256)
+        evidence(1, 256, 128)
+        evidence(1, 384, 128)

@@ -30,8 +30,7 @@ def tile_list_motif_variant_evidence_kernel(
     with ExitStack() as ctx:
         keep = ctx.enter_context(tc.tile_pool(name="keep", bufs=1))
         ring = ctx.enter_context(tc.tile_pool(name="ring", bufs=4))
-        diff_banks = ctx.enter_context(tc.psum_pool(name="diff_banks", bufs=6))
-        out_banks = ctx.enter_context(tc.psum_pool(name="out_banks", bufs=2))
+        psum = ctx.enter_context(tc.psum_pool(name="psum", bufs=8))
 
         def held(shape, dtype, name):
             return keep.tile(shape, dtype, name=name, align_bytes=64)
@@ -64,6 +63,8 @@ def tile_list_motif_variant_evidence_kernel(
         picked = {}
         grouped = {}
         mags = {}
+        diffs = {}
+        scores = {}
         damped = {}
 
         def load_plane(a, i):
@@ -77,7 +78,7 @@ def tile_list_motif_variant_evidence_kernel(
 
         def load_scale_rows(tile, rows):
             for q in range(4):
-                nc.scalar.dma_start(out=tile[32 * q : 32 * q + 4, :], in_=rows[0, 4 * q : 4 * q + 4, :].bitcast(I32))
+                nc.sync.dma_start(out=tile[32 * q : 32 * q + 4, :], in_=rows[0, 4 * q : 4 * q + 4, :].bitcast(I32))
 
         def cast(engine, out_ap, in_ap, factor):
             if engine == "scalar":
@@ -96,12 +97,14 @@ def tile_list_motif_variant_evidence_kernel(
             window = planes[a][i][:].indirect(x_list[:, j * LIST_COLS : (j + 1) * LIST_COLS])
             nc.vector.tensor_tensor(picked[a, j][:, i, :], window, wgt_sb[:, j * HALF : (j + 1) * HALF], MULT)
 
-        def group_xg(a, j, engine):
-            grouped["xg", a, j] = ring.tile([P, HALF * PACK], BF16, name=f"xg_bf{a}{j}", tag="grouped", align_bytes=64)
+        def group_xg(a, j, part, engine):
+            if ("xg", a, j) not in grouped:
+                grouped["xg", a, j] = ring.tile([P, HALF * PACK], BF16, name=f"xg_bf{a}{j}", tag="grouped", align_bytes=64)
+            c0, c1 = part * HALF // 2, (part + 1) * HALF // 2
             cast(
                 engine,
-                grouped["xg", a, j][:].rearrange("p (c u i) -> p c i u", u=4, i=PACK),
-                picked[a, j][:].rearrange("p i (c u) -> p c i u", u=4),
+                grouped["xg", a, j][:, PACK * c0 : PACK * c1].rearrange("p (c u i) -> p c i u", u=4, i=PACK),
+                picked[a, j][:, :, c0:c1].rearrange("p i (c u) -> p c i u", u=4),
                 -1.0,
             )
 
@@ -142,45 +145,36 @@ def tile_list_motif_variant_evidence_kernel(
             window = tab_w[:].bitcast(U32).indirect(tab_list[:, j * LIST_COLS : (j + 1) * LIST_COLS])
             nc.vector.tensor_copy(v_w[:, cols], window)
 
-        def difference(r, j, by_pass):
+        def difference(r, j, order, by_pass):
             sites = slice(j * HALF, (j + 1) * HALF)
             mags[r, j] = ring.tile([P, PACK, HALF], F32, name=f"mag{r}{j}", tag="wide_a", align_bytes=64)
-            banks = [diff_banks.tile([P, HALF], F32, name=f"diff{r}{j}{t}", tag="diff") for t in range(PACK)]
-
-            def sample_pass(t, a):
-                cols = slice(t * P, (t + 1) * P)
-                nc.tensor.matmul_mx(
-                    out=banks[t][:],
-                    lhsT=wk_w[a][r][:, cols].bitcast(FP8X4),
-                    lhsT_scale=wk_s[a][r][:, cols],
-                    rhs=xg_w[a][j][:].bitcast(FP8X4),
-                    rhs_scale=xg_s[a][j][:],
-                    start=(a == 0),
-                    stop=(a == 1),
-                )
-
-            def motif_pass(t):
-                c0 = r * HALF + t * P
-                nc.tensor.matmul_mx(
-                    out=banks[t][:],
-                    lhsT=wr_w[:, 2 * c0 : 2 * (c0 + P)].bitcast(FP4X4),
-                    lhsT_scale=wr_s[:, c0 : c0 + P],
-                    rhs=v_w[:, sites].bitcast(FP8X4),
-                    rhs_scale=v_s[:, sites],
-                    start=False,
-                    stop=False,
-                )
-
+            diffs[r, j] = [psum.tile([P, HALF], F32, name=f"diff{r}{j}{t}", tag="bank") for t in range(PACK)]
             steps = [(t, step) for t in range(PACK) for step in range(3)]
             if by_pass:
                 steps = [(t, step) for step in range(3) for t in range(PACK)]
             for t, step in steps:
-                if step == 1:
-                    motif_pass(t)
+                cols = slice(t * P, (t + 1) * P)
+                c0 = r * HALF + t * P
+                a = order[step]
+                if a == "motif":
+                    operands = (
+                        wr_w[:, 2 * c0 : 2 * (c0 + P)].bitcast(FP4X4),
+                        wr_s[:, c0 : c0 + P],
+                        v_w[:, sites].bitcast(FP8X4),
+                        v_s[:, sites],
+                    )
                 else:
-                    sample_pass(t, step // 2)
-                if step == 2:
-                    nc.scalar.activation(mags[r, j][:, t, :], banks[t][:], ACT.Abs)
+                    operands = (
+                        wk_w[a][r][:, cols].bitcast(FP8X4),
+                        wk_s[a][r][:, cols],
+                        xg_w[a][j][:].bitcast(FP8X4),
+                        xg_s[a][j][:],
+                    )
+                nc.tensor.matmul_mx(diffs[r, j][t][:], *operands, start=(step == 0), stop=(step == 2))
+
+        def magnitude(r, j, c0, width):
+            for t in range(PACK):
+                nc.scalar.activation(mags[r, j][:, t, c0 : c0 + width], diffs[r, j][t][:, c0 : c0 + width], ACT.Abs)
 
         def damp(r, j, c0, width):
             if (r, j) not in damped:
@@ -202,45 +196,74 @@ def tile_list_motif_variant_evidence_kernel(
             cols = slice(c0, c0 + width)
             quantize(h_w[r][j][:, cols], h_s[r][j][:, cols], grouped["h", r, j][:, PACK * c0 : PACK * (c0 + width)])
 
-        def evidence(j, c0, width):
+        def evidence_pass(target, n, r, j, c0, width):
             cols = slice(c0, c0 + width)
-            bank = out_banks.tile([P, 2, 256], F32, name=f"ev{j}_{c0}", tag="ev")
+            nc.tensor.matmul_mx(
+                out=target,
+                lhsT=wo_w[:, r, n * P : (n + 1) * P].bitcast(FP8X4),
+                lhsT_scale=wo_s[:, r, n * P : (n + 1) * P],
+                rhs=h_w[r][j][:, cols].bitcast(FP8X4),
+                rhs_scale=h_s[r][j][:, cols],
+                start=(r == 0),
+                stop=(r == 1),
+            )
+
+        def open_rows(n, j, c0, width):
+            scores[n, j, c0] = psum.tile([P, width], F32, name=f"rows{n}{j}_{c0}", tag="bank")
+            evidence_pass(scores[n, j, c0][:], n, 0, j, c0, width)
+
+        def close_rows(n, j, c0, width):
+            evidence_pass(scores[n, j, c0][:], n, 1, j, c0, width)
+
+        def store_rows(n, j, c0, width, engine):
+            staged = ring.tile([P, width], F32, name=f"staged{n}{j}_{c0}", tag="staged", bufs=6)
+            target = out[n * P : (n + 1) * P, j * HALF + c0 : j * HALF + c0 + width]
+            if engine == "scalar":
+                nc.scalar.copy(staged[:], scores[n, j, c0][:])
+                nc.scalar.dma_start(out=target, in_=staged[:])
+            else:
+                nc.vector.tensor_copy(staged[:], scores[n, j, c0][:])
+                nc.sync.dma_start(out=target, in_=staged[:])
+
+        def both_rows(j, c0, width):
+            scores[j, c0] = psum.tile([P, 2, width], F32, name=f"pair{j}_{c0}", tag="bank")
             for n in range(2):
                 for r in range(2):
-                    nc.tensor.matmul_mx(
-                        out=bank[:, n, :width],
-                        lhsT=wo_w[:, r, n * P : (n + 1) * P].bitcast(FP8X4),
-                        lhsT_scale=wo_s[:, r, n * P : (n + 1) * P],
-                        rhs=h_w[r][j][:, cols].bitcast(FP8X4),
-                        rhs_scale=h_s[r][j][:, cols],
-                        start=(r == 0),
-                        stop=(r == 1),
-                    )
-            staged = ring.tile([P, 2, 256], F32, name=f"staged{j}_{c0}", tag="staged")
-            nc.scalar.copy(staged[:, :, :width], bank[:, :, :width])
+                    evidence_pass(scores[j, c0][:, n, :], n, r, j, c0, width)
+
+        def store_both(j, c0, width, engine):
+            staged = ring.tile([P, 2, width], F32, name=f"staged{j}_{c0}", tag="staged", bufs=6)
             sites = slice(j * HALF + c0, j * HALF + c0 + width)
-            nc.sync.dma_start(out=out[:, sites].rearrange("(n p) s -> p n s", p=P), in_=staged[:, :, :width])
+            if engine == "scalar":
+                nc.scalar.copy(staged[:], scores[j, c0][:])
+            else:
+                nc.vector.tensor_copy(staged[:], scores[j, c0][:])
+            nc.sync.dma_start(out=out[:, sites].rearrange("(n p) s -> p n s", p=P), in_=staged[:])
+
+        def load_wgt(j):
+            nc.sync.dma_start(out=wgt_sb[:, j * HALF : (j + 1) * HALF], in_=wgt[:, j * HALF : (j + 1) * HALF])
 
         nc.vector.memset(tab_s[:], 0)
-        nc.vector.memset(wr_s_raw[:], 0)
         nc.vector.memset(ones[:], 1.0)
-        load_scale_rows(tab_s, tab_scales)
+        nc.vector.memset(wr_s_raw[:], 0)
         nc.scalar.activation(warm[:], ones[:], ACT.Ln)
-        load_scale_rows(wr_s_raw, wr_scales)
 
-        nc.sync.dma_start(x_list[:], offs2)
+        load_scale_rows(tab_s, tab_scales)
         nc.sync.dma_start(tab_list[:], offs)
-        nc.sync.dma_start(out=wgt_sb[:], in_=wgt)
+        nc.sync.dma_start(x_list[:], offs2)
+        load_wgt(0)
         load_plane(0, 0)
+        load_wgt(1)
         load_plane(0, 1)
-        nc.sync.dma_start(out=wr_w_raw[:], in_=wr_words[0].bitcast(I32))
         load_plane(0, 2)
+        load_scale_rows(wr_s_raw, wr_scales)
         load_plane(0, 3)
-        load_wk(0, 0)
+        nc.sync.dma_start(out=wr_w_raw[:], in_=wr_words[0].bitcast(I32))
         load_plane(1, 0)
+        load_wk(0, 0)
         load_plane(1, 1)
-        load_wk(1, 0)
         load_plane(1, 2)
+        load_wk(1, 0)
         load_plane(1, 3)
         nc.sync.dma_start(out=tab_w[:], in_=tab_words[0].rearrange("p t i -> p (t i)").bitcast(I32))
         nc.sync.dma_start(out=gain_sb[:], in_=gain.rearrange("(r p t) -> p r t", p=P, t=PACK))
@@ -255,64 +278,85 @@ def tile_list_motif_variant_evidence_kernel(
         nc.vector.tensor_copy(v_s[:], tab_s[:].bitcast(U8).indirect(tab_list[:]))
         both_halves(0, 0)
         both_halves(0, 1)
-        nc.vector.tensor_copy(
-            wr_w[:].bitcast(U16).rearrange("p (r t m) -> p r m t", r=2, t=PACK),
-            wr_w_raw[:].bitcast(U16).rearrange("p (r m t) -> p r m t", r=2, t=PACK),
-        )
+        both_halves(0, 2)
+        both_halves(0, 3)
+        for j in range(2):
+            for part in range(2):
+                group_xg(0, j, part, "scalar")
         nc.vector.tensor_copy(
             wr_s[:].rearrange("p (r t m) -> p r m t", r=2, t=PACK),
             wr_s_raw[:].bitcast(U8).rearrange("p (r m t) -> p r m t", r=2, t=PACK),
         )
-        both_halves(0, 2)
-        both_halves(0, 3)
-        group_xg(0, 0, "scalar")
-        group_xg(0, 1, "scalar")
-        group_wk(0, 0, "scalar")
-        group_wk(1, 0, "scalar")
+        nc.vector.tensor_copy(
+            wr_w[:].bitcast(U16).rearrange("p (r t m) -> p r m t", r=2, t=PACK),
+            wr_w_raw[:].bitcast(U16).rearrange("p (r m t) -> p r m t", r=2, t=PACK),
+        )
         both_halves(1, 0)
         quantize_xg(0, 0)
+        group_wk(0, 0, "scalar")
         both_halves(1, 1)
         quantize_xg(0, 1)
-        quantize_wk(0, 0)
         both_halves(1, 2)
-        quantize_wk(1, 0)
+        quantize_wk(0, 0)
+        group_wk(1, 0, "scalar")
         both_halves(1, 3)
-        group_xg(1, 0, "scalar")
+        group_xg(1, 0, 0, "scalar")
+        group_xg(1, 0, 1, "scalar")
+        quantize_wk(1, 0)
         gather_table_words(0)
         quantize_xg(1, 0)
-        difference(0, 0, True)
+        group_xg(1, 1, 0, "scalar")
+        group_xg(1, 1, 1, "scalar")
+        difference(0, 0, (0, "motif", 1), True)
+        magnitude(0, 0, 0, 512)
         damp(0, 0, 0, 512)
-        group_xg(1, 1, "vector")
         gather_table_words(1)
         quantize_xg(1, 1)
-        difference(0, 1, False)
-        damp(0, 1, 0, 512)
+        difference(0, 1, (0, "motif", 1), False)
+        magnitude(0, 1, 0, 512)
         group_wk(0, 1, "vector")
         group_wk(1, 1, "vector")
         quantize_wk(0, 1)
         quantize_wk(1, 1)
-        difference(1, 0, False)
-        damp(1, 0, 0, 512)
-        weigh(0, 0, 0, 512)
+        damp(0, 1, 0, 512)
+        difference(1, 0, (0, "motif", 1), False)
+        magnitude(1, 0, 0, 512)
         group_wo("vector")
-        quantize_h(0, 0, 0, 512)
+        weigh(0, 0, 0, 512)
         quantize_wo()
+        quantize_h(0, 0, 0, 512)
         weigh(0, 1, 0, 512)
-        difference(1, 1, False)
-        weigh(1, 0, 0, 512)
+        damp(1, 0, 0, 256)
+        damp(1, 0, 256, 256)
         quantize_h(0, 1, 0, 512)
-        quantize_h(1, 0, 0, 512)
+        difference(1, 1, (0, "motif", 1), False)
+        open_rows(0, 0, 0, 512)
+        open_rows(1, 0, 0, 512)
+        weigh(1, 0, 0, 256)
+        weigh(1, 0, 256, 256)
+        magnitude(1, 1, 0, 256)
         damp(1, 1, 0, 256)
+        magnitude(1, 1, 256, 256)
         damp(1, 1, 256, 128)
         damp(1, 1, 384, 128)
-        evidence(0, 0, 256)
-        evidence(0, 256, 256)
+        quantize_h(1, 0, 0, 512)
+        close_rows(0, 0, 0, 512)
+        close_rows(1, 0, 0, 512)
         weigh(1, 1, 0, 256)
-        weigh(1, 1, 256, 128)
+        store_rows(0, 0, 0, 512, "vector")
         quantize_h(1, 1, 0, 256)
+        open_rows(0, 1, 384, 128)
+        open_rows(1, 1, 384, 128)
+        both_rows(1, 0, 256)
+        weigh(1, 1, 256, 128)
         weigh(1, 1, 384, 128)
         quantize_h(1, 1, 256, 128)
         quantize_h(1, 1, 384, 128)
-        evidence(1, 0, 256)
-        evidence(1, 256, 128)
-        evidence(1, 384, 128)
+        both_rows(1, 256, 128)
+        close_rows(0, 1, 384, 128)
+        close_rows(1, 1, 384, 128)
+        store_rows(1, 0, 0, 512, "scalar")
+        store_both(1, 0, 256, "scalar")
+        store_both(1, 256, 128, "vector")
+        store_rows(0, 1, 384, 128, "scalar")
+        store_rows(1, 1, 384, 128, "vector")

@@ -55,8 +55,9 @@ def tile_list_motif_variant_evidence_kernel(
         wo_s = held([P, 2, N], U8, "wo_s")
         xg_w = [[held([P, HALF], U32, f"xg_w{a}{j}") for j in range(2)] for a in range(2)]
         xg_s = [[held([P, HALF], U8, f"xg_s{a}{j}") for j in range(2)] for a in range(2)]
-        wk_w = [[held([P, HALF], U32, f"wk_w{a}{r}") for r in range(2)] for a in range(2)]
-        wk_s = [[held([P, HALF], U8, f"wk_s{a}{r}") for r in range(2)] for a in range(2)]
+        wk_bf = [held([P, 2, HALF * PACK], BF16, f"wk_bf{r}") for r in range(2)]
+        wk_w = [held([P, 2, HALF], U32, f"wk_w{r}") for r in range(2)]
+        wk_s = [held([P, 2, HALF], U8, f"wk_s{r}") for r in range(2)]
         h_w = [[held([P, HALF], U32, f"h_w{r}{j}") for j in range(2)] for r in range(2)]
         h_s = [[held([P, HALF], U8, f"h_s{r}{j}") for j in range(2)] for r in range(2)]
         wk_raw = {}
@@ -99,7 +100,7 @@ def tile_list_motif_variant_evidence_kernel(
 
         def group_xg(a, j, part, engine):
             if ("xg", a, j) not in grouped:
-                grouped["xg", a, j] = ring.tile([P, HALF * PACK], BF16, name=f"xg_bf{a}{j}", tag="grouped", align_bytes=64)
+                grouped["xg", a, j] = ring.tile([P, HALF * PACK], BF16, name=f"xg_bf{a}{j}", tag="grouped", bufs=4, align_bytes=64)
             c0, c1 = part * HALF // 2, (part + 1) * HALF // 2
             cast(
                 engine,
@@ -111,20 +112,16 @@ def tile_list_motif_variant_evidence_kernel(
         def quantize_xg(a, j):
             quantize(xg_w[a][j][:], xg_s[a][j][:], grouped["xg", a, j][:])
 
-        def group_wk(a, r, engine):
-            grouped["wk", a, r] = ring.tile([P, HALF * PACK], BF16, name=f"wk_bf{a}{r}", tag="grouped", align_bytes=64)
+        def group_wk(a, r, target, engine):
             cast(
                 engine,
-                grouped["wk", a, r][:].rearrange("p (t m i) -> p m i t", t=PACK, i=PACK),
+                target.rearrange("p (t m i) -> p m i t", t=PACK, i=PACK),
                 wk_raw[a, r][:].rearrange("p i (m t) -> p m i t", t=PACK),
                 1.0,
             )
 
-        def quantize_wk(a, r):
-            quantize(wk_w[a][r][:], wk_s[a][r][:], grouped["wk", a, r][:])
-
         def group_wo(engine):
-            grouped["wo"] = ring.tile([P, 2, N * PACK], BF16, name="wo_bf", tag="grouped", align_bytes=64)
+            grouped["wo"] = ring.tile([P, 2, N * PACK], BF16, name="wo_bf", tag="grouped", bufs=4, align_bytes=64)
             for r in range(2):
                 cast(
                     engine,
@@ -165,15 +162,15 @@ def tile_list_motif_variant_evidence_kernel(
                     )
                 else:
                     operands = (
-                        wk_w[a][r][:, cols].bitcast(FP8X4),
-                        wk_s[a][r][:, cols],
+                        wk_w[r][:, a, cols].bitcast(FP8X4),
+                        wk_s[r][:, a, cols],
                         xg_w[a][j][:].bitcast(FP8X4),
                         xg_s[a][j][:],
                     )
                 nc.tensor.matmul_mx(diffs[r, j][t][:], *operands, start=(step == 0), stop=(step == 2))
 
-        def magnitude(r, j, c0, width):
-            for t in range(PACK):
+        def magnitude(r, j, c0, width, slots):
+            for t in slots:
                 nc.scalar.activation(mags[r, j][:, t, c0 : c0 + width], diffs[r, j][t][:, c0 : c0 + width], ACT.Abs)
 
         def damp(r, j, c0, width):
@@ -184,7 +181,7 @@ def tile_list_motif_variant_evidence_kernel(
 
         def weigh(r, j, c0, width):
             if ("h", r, j) not in grouped:
-                grouped["h", r, j] = ring.tile([P, HALF * PACK], BF16, name=f"h_bf{r}{j}", tag="grouped", align_bytes=64)
+                grouped["h", r, j] = ring.tile([P, HALF * PACK], BF16, name=f"h_bf{r}{j}", tag="grouped", bufs=4, align_bytes=64)
             nc.vector.tensor_tensor(
                 grouped["h", r, j][:, PACK * c0 : PACK * (c0 + width)].rearrange("p (c u t) -> p c t u", u=4, t=PACK),
                 damped[r, j][:, :, c0 : c0 + width].rearrange("p t (c u) -> p c t u", u=4),
@@ -220,7 +217,7 @@ def tile_list_motif_variant_evidence_kernel(
             target = out[n * P : (n + 1) * P, j * HALF + c0 : j * HALF + c0 + width]
             if engine == "scalar":
                 nc.scalar.copy(staged[:], scores[n, j, c0][:])
-                nc.scalar.dma_start(out=target, in_=staged[:])
+                (nc.scalar if j == 1 else nc.sync).dma_start(out=target, in_=staged[:])
             else:
                 nc.vector.tensor_copy(staged[:], scores[n, j, c0][:])
                 nc.sync.dma_start(out=target, in_=staged[:])
@@ -254,35 +251,37 @@ def tile_list_motif_variant_evidence_kernel(
         load_wgt(0)
         load_plane(0, 0)
         load_wgt(1)
-        load_plane(0, 1)
-        load_plane(0, 2)
-        load_scale_rows(wr_s_raw, wr_scales)
-        load_plane(0, 3)
-        nc.sync.dma_start(out=wr_w_raw[:], in_=wr_words[0].bitcast(I32))
-        load_plane(1, 0)
+        for a, i in [(0, 1), (0, 2), (0, 3), (1, 0), (1, 1), (1, 2)]:
+            load_plane(a, i)
         load_wk(0, 0)
-        load_plane(1, 1)
-        load_plane(1, 2)
+        load_scale_rows(wr_s_raw, wr_scales)
         load_wk(1, 0)
+        nc.sync.dma_start(out=wr_w_raw[:], in_=wr_words[0].bitcast(I32))
         load_plane(1, 3)
         nc.sync.dma_start(out=tab_w[:], in_=tab_words[0].rearrange("p t i -> p (t i)").bitcast(I32))
-        nc.sync.dma_start(out=gain_sb[:], in_=gain.rearrange("(r p t) -> p r t", p=P, t=PACK))
         load_wk(0, 1)
         load_wk(1, 1)
         nc.sync.dma_start(out=wo_raw[:], in_=wo.rearrange("(r p i) n -> p r i n", p=P, i=PACK))
+        nc.sync.dma_start(out=gain_sb[:], in_=gain.rearrange("(r p t) -> p r t", p=P, t=PACK))
 
         def both_halves(a, i):
             gather_plane(a, i, 0)
             gather_plane(a, i, 1)
 
         nc.vector.tensor_copy(v_s[:], tab_s[:].bitcast(U8).indirect(tab_list[:]))
-        both_halves(0, 0)
-        both_halves(0, 1)
-        both_halves(0, 2)
-        both_halves(0, 3)
+        for i in range(PACK):
+            both_halves(0, i)
         for j in range(2):
             for part in range(2):
                 group_xg(0, j, part, "scalar")
+        both_halves(1, 0)
+        quantize_xg(0, 0)
+        both_halves(1, 1)
+        quantize_xg(0, 1)
+        both_halves(1, 2)
+        group_wk(0, 0, wk_bf[0][:, 0, :], "scalar")
+        group_wk(1, 0, wk_bf[0][:, 1, :], "scalar")
+        quantize(wk_w[0][:, 0, :], wk_s[0][:, 0, :], wk_bf[0][:, 0, :])
         nc.vector.tensor_copy(
             wr_s[:].rearrange("p (r t m) -> p r m t", r=2, t=PACK),
             wr_s_raw[:].bitcast(U8).rearrange("p (r m t) -> p r m t", r=2, t=PACK),
@@ -291,70 +290,72 @@ def tile_list_motif_variant_evidence_kernel(
             wr_w[:].bitcast(U16).rearrange("p (r t m) -> p r m t", r=2, t=PACK),
             wr_w_raw[:].bitcast(U16).rearrange("p (r m t) -> p r m t", r=2, t=PACK),
         )
-        both_halves(1, 0)
-        quantize_xg(0, 0)
-        group_wk(0, 0, "scalar")
-        both_halves(1, 1)
-        quantize_xg(0, 1)
-        both_halves(1, 2)
-        quantize_wk(0, 0)
-        group_wk(1, 0, "scalar")
+        quantize(wk_w[0][:, 1, :], wk_s[0][:, 1, :], wk_bf[0][:, 1, :])
         both_halves(1, 3)
-        group_xg(1, 0, 0, "scalar")
-        group_xg(1, 0, 1, "scalar")
-        quantize_wk(1, 0)
+        for j in range(2):
+            for part in range(2):
+                group_xg(1, j, part, "scalar")
         gather_table_words(0)
-        quantize_xg(1, 0)
-        group_xg(1, 1, 0, "scalar")
-        group_xg(1, 1, 1, "scalar")
-        difference(0, 0, (0, "motif", 1), True)
-        magnitude(0, 0, 0, 512)
-        damp(0, 0, 0, 512)
         gather_table_words(1)
+        quantize_xg(1, 0)
         quantize_xg(1, 1)
+        difference(0, 0, (0, "motif", 1), True)
         difference(0, 1, (0, "motif", 1), False)
-        magnitude(0, 1, 0, 512)
-        group_wk(0, 1, "vector")
-        group_wk(1, 1, "vector")
-        quantize_wk(0, 1)
-        quantize_wk(1, 1)
-        damp(0, 1, 0, 512)
-        difference(1, 0, (0, "motif", 1), False)
-        magnitude(1, 0, 0, 512)
+        group_wk(0, 1, wk_bf[1][:, 0, :], "vector")
+        group_wk(1, 1, wk_bf[1][:, 1, :], "vector")
+        quantize(
+            wk_w[1][:].rearrange("p a c -> p (a c)"),
+            wk_s[1][:].rearrange("p a c -> p (a c)"),
+            wk_bf[1][:].rearrange("p a c -> p (a c)"),
+        )
         group_wo("vector")
+
+        magnitude(0, 0, 0, 512, range(4))
+        magnitude(0, 1, 0, 512, range(1))
+        damp(0, 0, 0, 512)
+        difference(1, 0, (0, "motif", 1), False)
+        magnitude(0, 1, 0, 512, range(1, 4))
+        magnitude(1, 0, 0, 512, range(1))
+        damp(0, 1, 0, 512)
+        difference(1, 1, (0, "motif", 1), False)
+        magnitude(1, 0, 0, 512, range(1, 4))
+        magnitude(1, 1, 0, 256, range(1))
+        damp(1, 0, 0, 256)
+        magnitude(1, 1, 0, 256, range(1, 3))
+        damp(1, 0, 256, 256)
+        magnitude(1, 1, 0, 256, range(3, 4))
+        magnitude(1, 1, 256, 256, range(1))
+        damp(1, 1, 0, 256)
+        magnitude(1, 1, 256, 256, range(1, 4))
+        damp(1, 1, 256, 128)
+        damp(1, 1, 384, 128)
+
         weigh(0, 0, 0, 512)
         quantize_wo()
         quantize_h(0, 0, 0, 512)
         weigh(0, 1, 0, 512)
-        damp(1, 0, 0, 256)
-        damp(1, 0, 256, 256)
-        quantize_h(0, 1, 0, 512)
-        difference(1, 1, (0, "motif", 1), False)
-        open_rows(0, 0, 0, 512)
-        open_rows(1, 0, 0, 512)
         weigh(1, 0, 0, 256)
+        quantize_h(0, 1, 0, 512)
         weigh(1, 0, 256, 256)
-        magnitude(1, 1, 0, 256)
-        damp(1, 1, 0, 256)
-        magnitude(1, 1, 256, 256)
-        damp(1, 1, 256, 128)
-        damp(1, 1, 384, 128)
-        quantize_h(1, 0, 0, 512)
-        close_rows(0, 0, 0, 512)
-        close_rows(1, 0, 0, 512)
         weigh(1, 1, 0, 256)
-        store_rows(0, 0, 0, 512, "vector")
-        quantize_h(1, 1, 0, 256)
-        open_rows(0, 1, 384, 128)
-        open_rows(1, 1, 384, 128)
-        both_rows(1, 0, 256)
         weigh(1, 1, 256, 128)
         weigh(1, 1, 384, 128)
+        quantize_h(1, 1, 0, 256)
         quantize_h(1, 1, 256, 128)
         quantize_h(1, 1, 384, 128)
+        quantize_h(1, 0, 0, 512)
+
+        open_rows(0, 0, 0, 512)
+        open_rows(1, 0, 0, 512)
+        open_rows(0, 1, 384, 128)
+        open_rows(1, 1, 384, 128)
+        close_rows(0, 0, 0, 512)
+        close_rows(1, 0, 0, 512)
+        both_rows(1, 0, 256)
         both_rows(1, 256, 128)
         close_rows(0, 1, 384, 128)
         close_rows(1, 1, 384, 128)
+        store_rows(0, 0, 0, 512, "scalar")
         store_rows(1, 0, 0, 512, "scalar")
         store_both(1, 0, 256, "scalar")
         store_both(1, 256, 128, "vector")

from contextlib import ExitStack

import concourse.mybir as mybir

K, M, H, N, T, S = 1024, 512, 1024, 256, 2048, 1024
FLOPS = 2 * S * (K * H + M * H + H * N)

F32 = mybir.dt.float32
BF16 = mybir.dt.bfloat16
I32 = mybir.dt.int32
U32 = mybir.dt.uint32
U16 = mybir.dt.uint16
U8 = mybir.dt.uint8
FP8X4 = mybir.dt.float8_e4m3fn_x4
FP4X4 = mybir.dt.float4_e2m1fn_x4
ACT = mybir.ActivationFunctionType
MULT = mybir.AluOpType.mult

P = 128
PACK = 4
PASS = P * PACK
HALF = 512
LIST_COLS = HALF // 16


def tile_list_motif_variant_evidence_kernel(
    tc, xT, wgt, offs2, tab_words, tab_scales, offs, wk, wr_words, wr_scales, gain, wo, out
):
    nc = tc.nc
    with ExitStack() as ctx:
        keep = ctx.enter_context(tc.tile_pool(name="keep", bufs=1))
        ring = ctx.enter_context(tc.tile_pool(name="ring", bufs=4))
        psum = ctx.enter_context(tc.psum_pool(name="psum", bufs=8))

        def held(shape, dtype, name):
            return keep.tile(shape, dtype, name=name, align_bytes=64)

        x_list = keep.tile([P, S // 16], U16, name="x_list")
        tab_list = keep.tile([P, S // 16], U16, name="tab_list")
        wgt_sb = held([P, S], F32, "wgt_sb")
        planes = [[held([P, T], F32, f"plane{a}{i}") for i in range(PACK)] for a in range(2)]
        tab_w = held([P, T], I32, "tab_w")
        tab_s = held([P, T // 4], I32, "tab_s")
        wr_w_raw = held([P, H // 2], I32, "wr_w_raw")
        wr_s_raw = held([P, H // 4], I32, "wr_s_raw")
        wr_w = held([P, 2 * H], U8, "wr_w")
        wr_s = held([P, H], U8, "wr_s")
        v_w = held([P, S], U32, "v_w")
        v_s = held([P, S], U8, "v_s")
        gain_sb = held([P, 2, PACK], F32, "gain_sb")
        ones = held([P, 1], F32, "ones")
        warm = held([P, 1], F32, "warm")
        wo_raw = held([P, 2, PACK, N], F32, "wo_raw")
        wo_w = held([P, 2, N], U32, "wo_w")
        wo_s = held([P, 2, N], U8, "wo_s")
        xg_w = [[held([P, HALF], U32, f"xg_w{a}{j}") for j in range(2)] for a in range(2)]
        xg_s = [[held([P, HALF], U8, f"xg_s{a}{j}") for j in range(2)] for a in range(2)]
        wk_bf = [held([P, 2, HALF * PACK], BF16, f"wk_bf{r}") for r in range(2)]
        wk_w = [held([P, 2, HALF], U32, f"wk_w{r}") for r in range(2)]
        wk_s = [held([P, 2, HALF], U8, f"wk_s{r}") for r in range(2)]
        h_w = [[held([P, HALF], U32, f"h_w{r}{j}") for j in range(2)] for r in range(2)]
        h_s = [[held([P, HALF], U8, f"h_s{r}{j}") for j in range(2)] for r in range(2)]
        wk_raw = {}
        picked = {}
        grouped = {}
        mags = {}
        diffs = {}
        scores = {}
        damped = {}

        def load_plane(a, i):
            rows = xT[a * PASS : (a + 1) * PASS, :].rearrange("(p i) t -> i p t", i=PACK)
            nc.sync.dma_start(out=planes[a][i][:], in_=rows[i])

        def load_wk(a, r):
            wk_raw[a, r] = ring.tile([P, PACK, HALF], F32, name=f"wk_raw{a}{r}", tag="wide_b", align_bytes=64)
            rows = wk[a * PASS : (a + 1) * PASS, r * HALF : (r + 1) * HALF]
            nc.sync.dma_start(out=wk_raw[a, r][:], in_=rows.rearrange("(p i) c -> p i c", i=PACK))

        def load_scale_rows(tile, rows):
            for q in range(4):
                nc.sync.dma_start(out=tile[32 * q : 32 * q + 4, :], in_=rows[0, 4 * q : 4 * q + 4, :].bitcast(I32))

        def cast(engine, out_ap, in_ap, factor):
            if engine == "scalar":
                nc.scalar.activation(out_ap, in_ap, ACT.Copy, scale=factor)
            elif factor == 1.0:
                nc.vector.tensor_copy(out_ap, in_ap)
            else:
                nc.vector.tensor_scalar(out_ap, in_ap, factor, None, MULT)

        def quantize(words, scales, grouped):
            nc.vector.quantize_mx(out=words.bitcast(FP8X4), scales=scales, in_=grouped)

        def gather_plane(a, i, j):
            if (a, j) not in picked:
                picked[a, j] = ring.tile([P, PACK, HALF], F32, name=f"picked{a}{j}", tag="wide_a", align_bytes=64)
            window = planes[a][i][:].indirect(x_list[:, j * LIST_COLS : (j + 1) * LIST_COLS])
            nc.vector.tensor_tensor(picked[a, j][:, i, :], window, wgt_sb[:, j * HALF : (j + 1) * HALF], MULT)

        def group_xg(a, j, part, engine):
            if ("xg", a, j) not in grouped:
                grouped["xg", a, j] = ring.tile([P, HALF * PACK], BF16, name=f"xg_bf{a}{j}", tag="grouped", bufs=4, align_bytes=64)
            c0, c1 = part * HALF // 2, (part + 1) * HALF // 2
            cast(
                engine,
                grouped["xg", a, j][:, PACK * c0 : PACK * c1].rearrange("p (c u i) -> p c i u", u=4, i=PACK),
                picked[a, j][:, :, c0:c1].rearrange("p i (c u) -> p c i u", u=4),
                -1.0,
            )

        def quantize_xg(a, j):
            quantize(xg_w[a][j][:], xg_s[a][j][:], grouped["xg", a, j][:])

        def group_wk(a, r, target, engine):
            cast(
                engine,
                target.rearrange("p (t m i) -> p m i t", t=PACK, i=PACK),
                wk_raw[a, r][:].rearrange("p i (m t) -> p m i t", t=PACK),
                1.0,
            )

        def group_wo(engine):
            grouped["wo"] = ring.tile([P, 2, N * PACK], BF16, name="wo_bf", tag="grouped", bufs=4, align_bytes=64)
            for r in range(2):
                cast(
                    engine,
                    grouped["wo"][:, r, :].rearrange("p (c u i) -> p c i u", u=4, i=PACK),
                    wo_raw[:, r, :, :].rearrange("p i (c u) -> p c i u", u=4),
                    1.0,
                )

        def quantize_wo():
            quantize(
                wo_w[:].rearrange("p r n -> p (r n)"),
                wo_s[:].rearrange("p r n -> p (r n)"),
                grouped["wo"][:].rearrange("p r c -> p (r c)"),
            )

        def gather_table_words(j):
            cols = slice(j * HALF, (j + 1) * HALF)
            window = tab_w[:].bitcast(U32).indirect(tab_list[:, j * LIST_COLS : (j + 1) * LIST_COLS])
            nc.vector.tensor_copy(v_w[:, cols], window)

        def difference(r, j, order, by_pass):
            sites = slice(j * HALF, (j + 1) * HALF)
            mags[r, j] = ring.tile([P, PACK, HALF], F32, name=f"mag{r}{j}", tag="wide_a", align_bytes=64)
            diffs[r, j] = [psum.tile([P, HALF], F32, name=f"diff{r}{j}{t}", tag="bank") for t in range(PACK)]
            steps = [(t, step) for t in range(PACK) for step in range(3)]
            if by_pass:
                steps = [(t, step) for step in range(3) for t in range(PACK)]
            for t, step in steps:
                cols = slice(t * P, (t + 1) * P)
                c0 = r * HALF + t * P
                a = order[step]
                if a == "motif":
                    operands = (
                        wr_w[:, 2 * c0 : 2 * (c0 + P)].bitcast(FP4X4),
                        wr_s[:, c0 : c0 + P],
                        v_w[:, sites].bitcast(FP8X4),
                        v_s[:, sites],
                    )
                else:
                    operands = (
                        wk_w[r][:, a, cols].bitcast(FP8X4),
                        wk_s[r][:, a, cols],
                        xg_w[a][j][:].bitcast(FP8X4),
                        xg_s[a][j][:],
                    )
                nc.tensor.matmul_mx(diffs[r, j][t][:], *operands, start=(step == 0), stop=(step == 2))

        def magnitude(r, j, c0, width, slots):
            for t in slots:
                nc.scalar.activation(mags[r, j][:, t, c0 : c0 + width], diffs[r, j][t][:, c0 : c0 + width], ACT.Abs)

        def damp(r, j, c0, width):
            if (r, j) not in damped:
                damped[r, j] = ring.tile([P, PACK, HALF], F32, name=f"damped{r}{j}", tag="wide_b", align_bytes=64)
            cols = slice(c0, c0 + width)
            nc.scalar.activation(damped[r, j][:, :, cols], mags[r, j][:, :, cols], ACT.Ln, bias=ones[:])

        def weigh(r, j, c0, width):
            if ("h", r, j) not in grouped:
                grouped["h", r, j] = ring.tile([P, HALF * PACK], BF16, name=f"h_bf{r}{j}", tag="grouped", bufs=4, align_bytes=64)
            nc.vector.tensor_tensor(
                grouped["h", r, j][:, PACK * c0 : PACK * (c0 + width)].rearrange("p (c u t) -> p c t u", u=4, t=PACK),
                damped[r, j][:, :, c0 : c0 + width].rearrange("p t (c u) -> p c t u", u=4),
                gain_sb[:, r, :].unsqueeze(1).unsqueeze(3).to_broadcast([P, width // 4, PACK, 4]),
                MULT,
            )

        def quantize_h(r, j, c0, width):
            cols = slice(c0, c0 + width)
            quantize(h_w[r][j][:, cols], h_s[r][j][:, cols], grouped["h", r, j][:, PACK * c0 : PACK * (c0 + width)])

        def evidence_pass(target, n, r, j, c0, width):
            cols = slice(c0, c0 + width)
            nc.tensor.matmul_mx(
                out=target,
                lhsT=wo_w[:, r, n * P : (n + 1) * P].bitcast(FP8X4),
                lhsT_scale=wo_s[:, r, n * P : (n + 1) * P],
                rhs=h_w[r][j][:, cols].bitcast(FP8X4),
                rhs_scale=h_s[r][j][:, cols],
                start=(r == 0),
                stop=(r == 1),
            )

        def open_rows(n, j, c0, width):
            scores[n, j, c0] = psum.tile([P, width], F32, name=f"rows{n}{j}_{c0}", tag="bank")
            evidence_pass(scores[n, j, c0][:], n, 0, j, c0, width)

        def close_rows(n, j, c0, width):
            evidence_pass(scores[n, j, c0][:], n, 1, j, c0, width)

        def store_rows(n, j, c0, width, engine):
            staged = ring.tile([P, width], F32, name=f"staged{n}{j}_{c0}", tag="staged", bufs=6)
            target = out[n * P : (n + 1) * P, j * HALF + c0 : j * HALF + c0 + width]
            if engine == "scalar":
                nc.scalar.copy(staged[:], scores[n, j, c0][:])
                (nc.scalar if j == 1 else nc.sync).dma_start(out=target, in_=staged[:])
            else:
                nc.vector.tensor_copy(staged[:], scores[n, j, c0][:])
                nc.sync.dma_start(out=target, in_=staged[:])

        def both_rows(j, c0, width):
            scores[j, c0] = psum.tile([P, 2, width], F32, name=f"pair{j}_{c0}", tag="bank")
            for n in range(2):
                for r in range(2):
                    evidence_pass(scores[j, c0][:, n, :], n, r, j, c0, width)

        def store_both(j, c0, width, engine):
            staged = ring.tile([P, 2, width], F32, name=f"staged{j}_{c0}", tag="staged", bufs=6)
            sites = slice(j * HALF + c0, j * HALF + c0 + width)
            if engine == "scalar":
                nc.scalar.copy(staged[:], scores[j, c0][:])
            else:
                nc.vector.tensor_copy(staged[:], scores[j, c0][:])
            nc.sync.dma_start(out=out[:, sites].rearrange("(n p) s -> p n s", p=P), in_=staged[:])

        def load_wgt(j):
            nc.sync.dma_start(out=wgt_sb[:, j * HALF : (j + 1) * HALF], in_=wgt[:, j * HALF : (j + 1) * HALF])

        nc.vector.memset(tab_s[:], 0)
        nc.vector.memset(ones[:], 1.0)
        nc.vector.memset(wr_s_raw[:], 0)
        nc.scalar.activation(warm[:], ones[:], ACT.Ln)

        load_scale_rows(tab_s, tab_scales)
        nc.sync.dma_start(tab_list[:], offs)
        nc.sync.dma_start(x_list[:], offs2)
        load_wgt(0)
        load_plane(0, 0)
        load_wgt(1)
        for a, i in [(0, 1), (0, 2), (0, 3), (1, 0), (1, 1), (1, 2)]:
            load_plane(a, i)
        load_wk(0, 0)
        load_scale_rows(wr_s_raw, wr_scales)
        load_wk(1, 0)
        nc.sync.dma_start(out=wr_w_raw[:], in_=wr_words[0].bitcast(I32))
        load_plane(1, 3)
        nc.sync.dma_start(out=tab_w[:], in_=tab_words[0].rearrange("p t i -> p (t i)").bitcast(I32))
        load_wk(0, 1)
        load_wk(1, 1)
        nc.sync.dma_start(out=wo_raw[:], in_=wo.rearrange("(r p i) n -> p r i n", p=P, i=PACK))
        nc.sync.dma_start(out=gain_sb[:], in_=gain.rearrange("(r p t) -> p r t", p=P, t=PACK))

        def both_halves(a, i):
            gather_plane(a, i, 0)
            gather_plane(a, i, 1)

        nc.vector.tensor_copy(v_s[:], tab_s[:].bitcast(U8).indirect(tab_list[:]))
        for i in range(PACK):
            both_halves(0, i)
        for j in range(2):
            for part in range(2):
                group_xg(0, j, part, "scalar")
        both_halves(1, 0)
        quantize_xg(0, 0)
        both_halves(1, 1)
        quantize_xg(0, 1)
        both_halves(1, 2)
        group_wk(0, 0, wk_bf[0][:, 0, :], "scalar")
        group_wk(1, 0, wk_bf[0][:, 1, :], "scalar")
        quantize(wk_w[0][:, 0, :], wk_s[0][:, 0, :], wk_bf[0][:, 0, :])
        nc.vector.tensor_copy(
            wr_s[:].rearrange("p (r t m) -> p r m t", r=2, t=PACK),
            wr_s_raw[:].bitcast(U8).rearrange("p (r m t) -> p r m t", r=2, t=PACK),
        )
        nc.vector.tensor_copy(
            wr_w[:].bitcast(U16).rearrange("p (r t m) -> p r m t", r=2, t=PACK),
            wr_w_raw[:].bitcast(U16).rearrange("p (r m t) -> p r m t", r=2, t=PACK),
        )
        quantize(wk_w[0][:, 1, :], wk_s[0][:, 1, :], wk_bf[0][:, 1, :])
        both_halves(1, 3)
        for j in range(2):
            for part in range(2):
                group_xg(1, j, part, "scalar")
        gather_table_words(0)
        gather_table_words(1)
        quantize_xg(1, 0)
        quantize_xg(1, 1)
        difference(0, 0, (0, "motif", 1), True)
        difference(0, 1, (0, "motif", 1), False)
        group_wk(0, 1, wk_bf[1][:, 0, :], "vector")
        group_wk(1, 1, wk_bf[1][:, 1, :], "vector")
        quantize(
            wk_w[1][:].rearrange("p a c -> p (a c)"),
            wk_s[1][:].rearrange("p a c -> p (a c)"),
            wk_bf[1][:].rearrange("p a c -> p (a c)"),
        )
        group_wo("vector")

        magnitude(0, 0, 0, 512, range(4))
        magnitude(0, 1, 0, 512, range(1))
        damp(0, 0, 0, 512)
        difference(1, 0, (0, "motif", 1), False)
        magnitude(0, 1, 0, 512, range(1, 4))
        magnitude(1, 0, 0, 512, range(1))
        damp(0, 1, 0, 512)
        difference(1, 1, (0, "motif", 1), False)
        magnitude(1, 0, 0, 512, range(1, 4))
        magnitude(1, 1, 0, 256, range(1))
        damp(1, 0, 0, 256)
        magnitude(1, 1, 0, 256, range(1, 3))
        damp(1, 0, 256, 256)
        magnitude(1, 1, 0, 256, range(3, 4))
        magnitude(1, 1, 256, 256, range(1))
        damp(1, 1, 0, 256)
        magnitude(1, 1, 256, 256, range(1, 4))
        damp(1, 1, 256, 128)
        damp(1, 1, 384, 128)

        weigh(0, 0, 0, 512)
        quantize_wo()
        quantize_h(0, 0, 0, 512)
        weigh(0, 1, 0, 512)
        weigh(1, 0, 0, 256)
        quantize_h(0, 1, 0, 512)
        weigh(1, 0, 256, 256)
        weigh(1, 1, 0, 256)
        weigh(1, 1, 256, 128)
        weigh(1, 1, 384, 128)
        quantize_h(1, 1, 0, 256)
        quantize_h(1, 1, 256, 128)
        quantize_h(1, 1, 384, 128)
        quantize_h(1, 0, 0, 512)

        open_rows(0, 0, 0, 512)
        open_rows(1, 0, 0, 512)
        open_rows(0, 1, 384, 128)
        open_rows(1, 1, 384, 128)
        close_rows(0, 0, 0, 512)
        close_rows(1, 0, 0, 512)
        both_rows(1, 0, 256)
        both_rows(1, 256, 128)
        close_rows(0, 1, 384, 128)
        close_rows(1, 1, 384, 128)
        store_rows(0, 0, 0, 512, "scalar")
        store_rows(1, 0, 0, 512, "scalar")
        store_both(1, 0, 256, "scalar")
        store_both(1, 256, 128, "vector")
        store_rows(0, 1, 384, 128, "scalar")
        store_rows(1, 1, 384, 128, "vector")
